import numpy as np, ml_dtypes
CORES = [40,64,80,88,96,104,120,144]
N = 8
BF = ml_dtypes.bfloat16
def gentries(a):
    return np.ascontiguousarray(a.reshape(8, 16, -1).transpose(0, 2, 1)).reshape(8, -1)
def gtable(e):
    e = np.asarray(e); return np.ascontiguousarray(e.reshape(8, -1, 16).transpose(0, 2, 1)).reshape(128, -1).astype(np.int32)
def f(rng, *shape):
    return (rng.standard_normal(shape, dtype=np.float32) * np.exp2(rng.integers(-2, 3, shape[:-1] + (1,)))).astype(BF)
def wide(rng, *shape):
    v = f(rng, *shape).astype(np.float32); k = shape[:-2] + (1, shape[-1])
    return (v * np.exp2(rng.integers(-6, 7, k)) * (rng.random(k) > 0.0625)).astype(BF)
P, E, M, G = 3072, 4096, 256, 64
Z = P + (N - 1) * G
DX, DY = (-1, 0, 1, -1, 1, -1, 0, 1), (-1, -1, -1, 0, 0, 1, 1, 1)
FAR = [[(d, s) for d in range(8) for s in range(4) if max(abs(2 * DX[d] + s % 2 - c % 2), abs(2 * DY[d] + s // 2 - c // 2)) > 1] for c in range(4)]
def kids(rng):
    return rng.permuted(np.tile(np.minimum(np.arange(4 * P), E), (N, 8, 1)), axis=2).reshape(N, 8, 4, P)
def nears(rng, own, ghost):
    u = rng.random((N, 8, 8, M))
    return np.where(u < own, rng.integers(0, P, u.shape), np.where(u < own + ghost, rng.integers(P, Z, u.shape), Z))
def gives(rng):
    return rng.integers(0, P, (N, 8, N - 1, G))
def pack(rng, ki, ne, gi):
    return {"ex": f(rng, N, 128, E), "kid": ki.reshape(N, 8, 4 * P).astype(np.int32), "near": np.stack([gtable(a.reshape(8, 8 * M)) for a in ne]),
            "give": np.stack([gtable(a.reshape(8, (N - 1) * G)) for a in gi]), "tr": f(rng, N, 128, 108)}
def setup_inputs(rng):
    return pack(rng, kids(rng), nears(rng, 0.5, 0.42), gives(rng))
def setup_inputs_ghosts(rng):
    ne = nears(rng, 0.0, 2.0); q = rng.integers(0, N); ne[q] = P + G * rng.integers(0, N - 1) + rng.integers(0, G, (8, 8, M))
    for b in range(N - 1):
        ne[:, :, b, 0] = P + G * b; ne[:, :, b, M - 1] = P + G * b + G - 1
    return pack(rng, kids(rng), ne, gives(rng))
def setup_inputs_empty(rng):
    ne = nears(rng, 0.15, 0.15); ne[:, :, :, ::4] = Z; ne[:, rng.choice(np.array([0, 3, 4, 6, 7]))] = Z
    ki = kids(rng); ki[:, :, :, rng.random(P) < 0.5] = E; b = rng.integers(0, P)
    ki[:, :, :, b] = rng.integers(0, E, (N, 8, 4)); ne[:, 1:3, 0, 1] = b
    ne[:, 5, 7, 2] = b
    return pack(rng, ki, ne, gives(rng))
def setup_inputs_ends(rng):
    ne = rng.choice(np.array([0, P - 1, P, P + G - 1, Z - G, Z - 1, Z]), (N, 8, 8, M)); ki = kids(rng)
    for p in (0, P - 1): ki[:, :, :, p] = rng.permuted(np.tile(np.array([0, E - 1, E, E - 1]), (N, 8, 1)), axis=2)
    return pack(rng, ki, ne, rng.choice(np.array([0, P - 1]), (N, 8, N - 1, G)))
def setup_inputs_alike(rng):
    ne = np.tile(rng.integers(0, Z, (N, 8, 8, 1)), (1, 1, 1, M)); gi = np.tile(rng.integers(0, P, (N, 8, N - 1, 1)), (1, 1, 1, G))
    return pack(rng, rng.integers(0, E, (N, 8, 4, P)), ne, gi)
def setup_inputs_spread(rng):
    d = setup_inputs(rng); d["ex"] = wide(rng, N, 128, E); return d
def check_inputs(d):
    bad = []
    for a, top in (("kid", E), ("near", Z), ("give", P - 1)):
        if d[a].min() < 0 or d[a].max() > top: bad.append(a)
    for a in ("ex", "tr"):
        if not np.isfinite(d[a].astype(np.float32)).all(): bad.append(a)
    return bad
def reference(ex, kid, near, give, tr):
    x = np.concatenate([ex.astype(np.float64).reshape(N, 8, 16, E), np.zeros((N, 8, 16, 1))], 3)
    ch = kid.reshape(N, 8, 4, P); t = tr.astype(np.float64).reshape(N, 8, 16, 4, 27)
    gi = [gentries(a).reshape(8, N - 1, G) for a in give]; ne = [gentries(a).reshape(8, 8, M) for a in near]
    y = np.zeros((N, 8, 16, 4, M), np.float64)
    for r in range(N):
        for g in range(8):
            w = [x[r, g][:, ch[r, g]]]
            for d in range(1, N):
                q = (r - d) % N
                w.append(x[q, g][:, ch[q, g][:, gi[q][g, d - 1]]])
            w = np.concatenate(w + [np.zeros((16, 4, 1))], 2)
            v = w[:, :, ne[r][g]]
            for c in range(4):
                for i, (d, s) in enumerate(FAR[c]):
                    y[r, g, :, c] += t[r, g, :, c, i, None] * v[:, s, d]
    return {"y": y.reshape(N, 128, 4 * M).astype(np.float32)}

@@ -1,0 +1,397 @@
+from concourse.bass import DstId, RemoteDMATransfer
+from concourse.mybir import AluOpType, ActivationFunctionType
+
+P, E, M, G, N = 3072, 4096, 256, 64, 8
+Q = P // 4
+NG = (N - 1) * G
+GH = E + 16
+WEND = GH + 2 * NG + 16
+BW = 144
+NL = NG + 8 * M
+DX, DY = (-1, 0, 1, -1, 1, -1, 0, 1), (-1, -1, -1, 0, 0, 1, 1, 1)
+FAR = [[4 * d + s for d in range(8) for s in range(4)
+        if max(abs(2 * DX[d] + s % 2 - c % 2), abs(2 * DY[d] + s // 2 - c // 2)) > 1] for c in range(4)]
+
+XN_CHUNKS = 4
+XN_PRE = 1
+XN_MID = 3
+WT_ACT = 25
+WT_EARLY = 4
+HALVES = (1, 2)
+SPREAD = (True, False)
+RELAY_ENGINES = 8
+
+SCRATCH = {
+    "ex0": ("sbuf", [128, WEND], "bfloat16"),
+    "ex1": ("sbuf", [128, WEND], "bfloat16"),
+    "kn": ("sbuf", [128, Q], "int32"),
+    "kf": ("sbuf", [128, Q + NG + 8], "float32"),
+    "ng": ("sbuf", [128, NL // 16], "int32"),
+    "qi": ("sbuf", [128, NL // 16], "int32"),
+    "tq": ("sbuf", [128, NL // 16], "float32"),
+    "lo": ("sbuf", [128, NL // 16], "int32"),
+    "qu": ("sbuf", [128, NL // 16], "uint16"),
+    "lu": ("sbuf", [128, NL // 16], "uint16"),
+    "pi": ("sbuf", [128, 1], "int32"),
+    "ix": ("sbuf", [128, NG + 8], "float32"),
+    "ci": ("sbuf", [128, 8], "int32"),
+    "cf": ("sbuf", [128, 8], "float32"),
+    "ct": ("sbuf", [128, 8], "float32"),
+    "oh": ("sbuf", [128, 8], "float32"),
+    "big": ("sbuf", [128, 2 * BW], "float16"),
+    "i64f": ("sbuf", [128, 64], "float32"),
+    "i64b": ("sbuf", [128, 64], "bfloat16"),
+    "mk": ("sbuf", [128, NL], "bfloat16"),
+    "xs": ("sbuf", [128, NL], "float16"),
+    "og0": ("sbuf", [128, NG // 8], "uint16"),
+    "og1": ("sbuf", [128, NG // 8], "uint16"),
+    "on0": ("sbuf", [128, M], "uint16"),
+    "on1": ("sbuf", [128, M], "uint16"),
+    "gs0": ("sbuf", [128, 2 * NG], "bfloat16"),
+    "gs1": ("sbuf", [128, 2 * NG], "bfloat16"),
+    "rl0": ("sbuf", [128, 2 * G], "bfloat16"),
+    "rl1": ("sbuf", [128, 2 * G], "bfloat16"),
+    "trr": ("sbuf", [128, 2, 108], "bfloat16"),
+    "tf": ("sbuf", [128, 2, 2, 64], "bfloat16"),
+    "trw": ("sbuf", [128, 128], "bfloat16"),
+    "wt": ("sbuf", [128, 64 * 128], "bfloat16"),
+    "v0": ("sbuf", [128, 16 * M], "bfloat16"),
+    "v1": ("sbuf", [128, 16 * M], "bfloat16"),
+    "o0": ("sbuf", [128, 2 * M], "float32"),
+    "o1": ("sbuf", [128, 2 * M], "float32"),
+    "pg0": ("psum", [128, 512], "float32"),
+    "pg1": ("psum", [128, 512], "float32"),
+    "pn0": ("psum", [128, 16, 32], "float32"),
+    "pn1": ("psum", [128, 16, 32], "float32"),
+    "py00": ("psum", [128, 512], "float32"),
+    "py01": ("psum", [128, 512], "float32"),
+    "py10": ("psum", [128, 512], "float32"),
+    "py11": ("psum", [128, 512], "float32"),
+}
+NSEM = 120
+SEMAPHORES = ["arr0", "arr1", "rin0", "rin1", "sent"] + ["s%d" % i for i in range(NSEM)]
+
+
+def bits(engs):
+    m = 0
+    for e in engs:
+        m |= 1 << e
+    return m
+
+
+def pow2(n):
+    p = 1
+    while 2 * p <= n:
+        p *= 2
+    return p
+
+
+def routes(cores, topo):
+    out = []
+    n = len(cores)
+    for r, src in enumerate(cores):
+        dsts = [(d, cores[(r + d) % n]) for d in range(1, n)]
+        direct = [x for x in dsts if topo.may_write(src, x[1])]
+        cross = [x for x in dsts if not topo.may_write(src, x[1])]
+        cross.sort(key=lambda x: not topo.mates(src, x[1]))
+        used, hand = [], []
+        for d, dst in cross:
+            able = [c for c in topo.cores_of(src) if c not in cores and c not in used and topo.may_write(c, dst)]
+            able.sort(key=lambda c: topo.die(c) != topo.die(src))
+            used.append(able[0])
+            hand.append((d, able[0], dst))
+        near = [h for h in hand if topo.die(h[1]) == topo.die(src)]
+        far = [h for h in hand if topo.die(h[1]) != topo.die(src)]
+        off = list(topo.engines(src, direct[0][1])) if direct else []
+        mine = {h: [] for h in hand}
+        for w in range(2):
+            engs = [e for e in topo.engines(src, hand[0][1]) if SPREAD[w] or e not in off]
+            pools = ((near, engs[1::2]), (far, engs[0::2])) if near and far else ((hand, engs),)
+            for hs, pool in pools:
+                k = pow2(len(pool) // len(hs))
+                for i, h in enumerate(hs):
+                    mine[h].append(pool[i * k:(i + 1) * k])
+        rel = [(h[0], h[1], mine[h], h[2], topo.engines(h[1], h[2])[:RELAY_ENGINES]) for h in hand]
+        dire = []
+        for i, (d, dst) in enumerate(direct):
+            left = len(direct) - i
+            k = pow2(len(off) - (left - 1) * pow2(len(off) // left))
+            dire.append((d, dst, off[:k]))
+            off = off[k:]
+        out.append((dire, rel))
+    return out
+
+
+def runs(c):
+    f, out, i = FAR[c], [], 0
+    while i < len(f):
+        j = i
+        while j + 1 < len(f) and f[j + 1] == f[j] + 1:
+            j += 1
+        out.append((i, f[i], j - i + 1))
+        i = j + 1
+    return out
+
+
+def relay_program(g, core, T, topo, d, engs_in, dst, engs_out):
+    rid, pid = topo.addr(dst, core)
+    for w in range(2):
+        g.wait_ge(T.sem["rin%d" % w], len(engs_in[w]))
+        a = GH + 2 * G * (d - 1)
+        g.remote_dma(T["ex%d" % w][:, a:a + 2 * G], T["rl%d" % w][:], T.sem["arr%d" % w], T.sem.sent,
+                     pid, rid, bits(engs_out))
+    g.wait_ge(T.sem.sent, 2 * len(engs_out))
+
+
+def rank_program(g, core, T, topo):
+    plan = routes(list(T.cores), topo)
+    rank = T.rank_of(core)
+    if rank is None:
+        for dire, rel in plan:
+            for d, c, engs_in, dst, engs_out in rel:
+                if c == core:
+                    relay_program(g, core, T, topo, d, engs_in, dst, engs_out)
+        return
+    dire, rel = plan[rank]
+    arrive = sum(len(x[2]) for p in plan for x in p[0] if x[1] == core) \
+        + sum(len(x[4]) for p in plan for x in p[1] if x[3] == core)
+
+    V, A, PE, S = g.vector, g.scalar, g.tensor, g.sync
+    op, Copy = AluOpType, ActivationFunctionType.Copy
+    count = [0]
+
+    def mark():
+        count[0] += 1
+        return [T.sem["s%d" % (count[0] - 1)], 0]
+
+    def to(m, ins, n=1):
+        ins.then_inc(m[0], n)
+        m[1] += n
+        return m
+
+    def wait(q, *ms):
+        for m in ms:
+            q.wait_ge(m[0], m[1])
+
+    def copy(q, dst, src):
+        return V.tensor_copy(dst, src) if q is V else A.activation(dst, src, Copy)
+
+    ex, gs, og, on = (T.ex0, T.ex1), (T.gs0, T.gs1), (T.og0, T.og1), (T.on0, T.on1)
+    vv, oo, pg, pn = (T.v0, T.v1), (T.o0, T.o1), (T.pg0, T.pg1), (T.pn0, T.pn1)
+    py = (((T.py00, T.py01),), ((T.py10, T.py11), (T.pg0, T.pg1)))
+    GC = NG // 16
+
+    m_ng, m_kid, m_tr, m_ex = mark(), mark(), mark(), (mark(), mark())
+    to(m_ng, S.dma_start(T.ng[:, 0:GC], T.give[:]), 16)
+    to(m_ng, A.dma_start(T.ng[:, GC:], T.near[:]), 16)
+    to(m_kid, S.dma_start(T.kn[:], T.kid[:]), 16)
+    for k in range(2):
+        to(m_ex[0], S.dma_start(ex[0][64 * k:64 * k + 64, 0:E], T.ex[0:64, :]), 16)
+    for w in range(2):
+        for k in range(2):
+            to(m_tr, S.dma_start(T.trr[64 * k:64 * k + 64, w, :], T.tr[64 * w:64 * w + 64, :]), 16)
+    wait(S, m_kid)
+    for k in range(2):
+        to(m_ex[1], S.dma_start(ex[1][64 * k:64 * k + 64, 0:E], T.ex[64:128, :]), 16)
+
+    m_pi = to(mark(), g.iota(T.pi[:], [[1, 1]], 0, 1))
+    m_ix = to(mark(), g.iota(T.ix[:], [[1, NG + 8]], 0, 0, allow_small_or_imprecise_dtypes=True))
+    m_zero = mark()
+    for w in range(2):
+        to(m_zero, V.memset(ex[w][:, E:GH], 0.0))
+        to(m_zero, V.memset(ex[w][:, WEND - 16:WEND], 0.0))
+    to(m_zero, V.memset(T.tf[:], 0.0))
+    wait(V, m_pi)
+    m = mark()
+    for j, b in enumerate((3, 4, 8, 48, 64, 63)):
+        to(m, V.tensor_scalar(T.ci[:, j:j + 1], T.pi[:], b, None, op.bitwise_and))
+    wait(V, m)
+    m = to(mark(), V.tensor_copy(T.cf[:, 0:6], T.ci[:, 0:6]))
+    wait(V, m, m_ix)
+    cf = [T.cf[:, j:j + 1] for j in range(6)]
+    ct = [T.ct[:, j:j + 1] for j in range(4)]
+    m_oh = mark()
+    to(m_oh, V.tensor_scalar(ct[0], cf[1], 16.0, cf[3], op.mult, op.add))
+    to(m_oh, V.tensor_scalar(ct[1], cf[4], BW / 64.0, 14.0, op.mult, op.add))
+    to(m_oh, V.tensor_scalar(T.oh[:, 0:4], T.ix[:, 0:4], cf[0], None, op.is_equal))
+    to(m_oh, V.tensor_scalar(T.oh[:, 4:5], cf[0], 2.0, None, op.is_ge))
+    wait(V, m_oh)
+    m = mark()
+    to(m, V.tensor_scalar(ct[2], cf[2], 0.125, ct[1], op.mult, op.add))
+    to(m, V.tensor_scalar(ct[3], T.oh[:, 3:4], cf[2], 0.125, op.mult, op.mult))
+    wait(V, m)
+    m_big = to(mark(), V.tensor_scalar(T.big[:], T.ix[:, 0:2 * BW], ct[0], ct[2], op.subtract, op.is_equal))
+    m_kf = to(mark(), V.tensor_scalar(T.kf[:, Q:], T.ix[:], ct[3], (GH - E // 2) / 2.0, op.add, op.add))
+    m_i64 = mark()
+    to(m_i64, V.tensor_scalar(T.i64f[:], T.ix[:, 0:64], cf[5], None, op.is_equal))
+    to(m_i64, V.tensor_scalar(T.i64b[:], T.ix[:, 0:64], cf[5], None, op.is_equal))
+
+    wait(V, m_ng)
+    m = to(mark(), V.tensor_scalar(T.qi[:], T.ng[:], 1.0 / Q, 0.5 / Q - 0.5, op.mult, op.add))
+    wait(V, m)
+    m_qu = to(mark(), V.tensor_copy(T.qu[:], T.qi[:]))
+    m = to(mark(), V.tensor_scalar(T.tq[:], T.qi[:], 3.0, -float(Q), op.min, op.mult))
+    wait(V, m)
+    m = to(mark(), V.tensor_tensor(T.lo[:], T.ng[:], T.tq[:], op.add))
+    wait(V, m)
+    m_lu = to(mark(), V.tensor_copy(T.lu[:], T.lo[:]))
+
+    cw = 8 * M // 16 // XN_CHUNKS
+    spans = [(0, GC)] + [(GC + i * cw, GC + (i + 1) * cw) for i in range(XN_CHUNKS)]
+    wait(A, m_oh, m_qu)
+    m_mk = [to(mark(), A.activation(T.mk[:, 16 * a:16 * b], T.oh[:, 0:5].indirect(T.qu[:, a:b]), Copy))
+            for a, b in spans]
+
+    wait(V, m_kid)
+    to(m_kf, V.tensor_scalar(T.kf[:, 0:Q], T.kn[:], -float(E // 2), None, op.add))
+    wait(V, m_kf, m_lu)
+
+    def lookup(i, m):
+        a, b = spans[i]
+        wait(V, m_mk[i])
+        return to(m, V.tensor_tensor(T.xs[:, 16 * a:16 * b], T.kf[:].indirect(T.lu[:, a:b]),
+                                     T.mk[:, 16 * a:16 * b], op.mult))
+
+    def deal(ps, w, a, b):
+        for u in range(8):
+            c0 = BW * w + 14 - 2 * u
+            ins = PE.matmul(ps, T.big[:, c0:c0 + 128], T.xs[:, a + u:b:8], u == 0, u == 7)
+        return to(mark(), ins)
+
+    m_xg, m_xn = lookup(0, mark()), mark()
+    wait(PE, m_big, m_xg)
+    m_pg = [deal(pg[w][:, 0:NG // 8], w, 0, NG) for w in range(2)]
+    m_og = []
+    for w in range(2):
+        wait(V, m_pg[w])
+        m_og.append(to(mark(), V.tensor_scalar(og[w][:], pg[w][:, 0:NG // 8], float(E // 2), None, op.add)))
+    for i in range(XN_PRE):
+        lookup(1 + i, m_xn)
+
+    def ghosts(w):
+        for q in (V, A):
+            wait(q, m_og[w], m_ex[w])
+        sets = (sorted(x[0] for x in rel), sorted(x[0] for x in dire))
+        ms = (mark(), mark())
+        for ds, m in zip(sets, ms):
+            cols = [8 * (d - 1) + 4 * h for d in ds for h in range(2)]
+            for q, mine in ((V, cols[:len(ds)]), (A, cols[len(ds):])):
+                while mine:
+                    n = 1
+                    while n < len(mine) and mine[n] == mine[0] + 4 * n:
+                        n += 1
+                    a, b, mine = mine[0], mine[0] + 4 * n, mine[n:]
+                    to(m, copy(q, gs[w][:, 16 * a:16 * b], ex[w][:, 0:GH].indirect(og[w][:, a:b])))
+        blk = lambda d: gs[w][:, 2 * G * (d - 1):2 * G * d]
+        ident = lambda c: DstId(rid=topo.addr(c, core)[0], pnc=topo.addr(c, core)[1])
+        wait(g, ms[0])
+        g.remote_dma_fused([RemoteDMATransfer(dst_ids=[ident(c)], dma_engine_mask=bits(e[w]), remote_sem=T.sem["rin%d" % w],
+                                              src=blk(d), dst=T["rl%d" % w][:]) for d, c, e, _, _ in rel],
+                           local_sem=T.sem.sent)
+        wait(g, ms[1])
+        g.remote_dma_fused([RemoteDMATransfer(dst_ids=[ident(c)], dma_engine_mask=bits(e), remote_sem=T.sem["arr%d" % w],
+                                              src=blk(d), dst=ex[w][:, GH + 2 * G * (d - 1):GH + 2 * G * d])
+                            for d, c, e in dire], local_sem=T.sem.sent)
+
+    for q in (V, A):
+        wait(q, m_zero)
+    ghosts(0)
+
+    wait(A, m_tr)
+    m = mark()
+    for c in range(4):
+        for i0, p0, n in runs(c):
+            a = 32 * (c // 2) + p0
+            to(m, copy(A, T.tf[:, c % 2, :, a:a + n], T.trr[:, :, 27 * c + i0:27 * c + i0 + n]))
+    wait(A, m)
+    m_trw = mark()
+    for k in range(2):
+        to(m_trw, copy(A, T.trw[64 * k:64 * k + 64, :], T.tf[64 * k:64 * k + 64, :, :, k::2]))
+
+    m_wt = mark()
+
+    def blocks(q, es):
+        for e in es:
+            dst = T.wt[:, 128 * e:128 * e + 128]
+            if q is V:
+                to(m_wt, V.tensor_scalar(dst, T.trw[:], T.i64b[:, e:e + 1], None, op.mult))
+            else:
+                to(m_wt, A.activation(dst, T.trw[:], Copy, scale=T.i64f[:, e:e + 1]))
+
+    wait(A, m_trw, m_i64)
+    blocks(A, range(0, WT_EARLY))
+    for i in range(XN_PRE, XN_PRE + XN_MID):
+        lookup(1 + i, m_xn)
+    ghosts(1)
+    for i in range(XN_PRE + XN_MID, XN_CHUNKS):
+        lookup(1 + i, m_xn)
+    blocks(A, range(WT_EARLY, WT_ACT))
+    wait(PE, m_xn)
+    m_pn = [deal(pn[w][:, 0:8, :], w, NG, NL) for w in range(2)]
+    m_on = []
+    for w in range(2):
+        wait(V, m_pn[w])
+        m, hw = mark(), 32 // HALVES[w]
+        for h in range(HALVES[w]):
+            to(m, V.tensor_scalar(on[w][:, 8 * hw * h:8 * hw * (h + 1)], pn[w][:, 0:8, hw * h:hw * (h + 1)],
+                                  float(E // 2), None, op.add))
+        m_on.append(m)
+    wait(V, m_trw, m_i64)
+    blocks(V, range(WT_ACT, 64))
+    wait(PE, m_wt)
+
+    m_out = mark()
+
+    def store(w, h, done):
+        mh = M // HALVES[w]
+        for cp, q, dq in ((0, V, S), (1, A, A)):
+            b = M * cp + mh * h
+            wait(q, done[cp])
+            wait(dq, to(mark(), copy(q, oo[w][:, b:b + mh], py[w][h][cp][:, 0:mh])))
+            if HALVES[w] == 1:
+                to(m_out, dq.dma_start(T.y[64 * w:64 * w + 64, 2 * M * cp:2 * M * (cp + 1)], oo[w][:, b:b + mh]), 16)
+            else:
+                for c in range(2):
+                    a = 2 * M * cp + M * c + mh * h
+                    to(m_out, dq.dma_start(T.y[64 * w:64 * w + 64, a:a + mh], oo[w][c::2, b:b + mh]), 16)
+
+    pending, turn = [], 0
+    for w in range(2):
+        for q in (V, A):
+            wait(q, m_on[w])
+            q.wait_ge(T.sem["arr%d" % w], arrive)
+        H = HALVES[w]
+        mh, hw = M // H, 32 // H
+        passes = [[(d, s) for d in range(8) for s in range(2)
+                   if any(4 * d + 2 * s + k in FAR[c + 2 * cp] for k in range(2) for c in range(2))] for cp in range(2)]
+        for h in range(H):
+            done = [None, None]
+            for n in range(8 // H):
+                base = 8 * hw * h + 32 * n
+                m = mark()
+                if base == (0 if w == 0 else M - 32):
+                    parts = ((V, 0, 16), (A, 16, 32))
+                else:
+                    parts = (((A, V)[turn], 0, 32),)
+                    turn = 1 - turn
+                for q, a, b in parts:
+                    to(m, copy(q, vv[w][:, 16 * (base + a):16 * (base + b)],
+                               ex[w][:].indirect(on[w][:, base + a:base + b])))
+                if pending and n == min(3, 8 // H - 2):
+                    store(*pending.pop())
+                wait(PE, m)
+                for cp in range(2):
+                    for d in range(H * n, H * (n + 1)):
+                        for s in range(2):
+                            if (d, s) in passes[cp]:
+                                j = ((2 * w + cp) * 8 + d) * 2 + s
+                                a = 16 * (8 * hw * h + hw * d)
+                                ins = PE.matmul(py[w][h][cp][:, 0:mh], T.wt[:, j::64],
+                                                vv[w][:, a + s:a + 2 * mh:2],
+                                                (d, s) == passes[cp][0], (d, s) == passes[cp][-1])
+                                if (d, s) == passes[cp][-1]:
+                                    done[cp] = to(mark(), ins)
+            pending.append((w, h, done))
+    store(*pending.pop())
+    wait(S, m_out)
+    g.wait_ge(T.sem.sent, sum(len(x[2][0]) + len(x[2][1]) for x in rel) + 2 * sum(len(x[2]) for x in dire))

@@ -2,7 +2,6 @@ from concourse.bass import DstId, RemoteDMATransfer
 from concourse.mybir import AluOpType, ActivationFunctionType
 
 P, E, M, G, N = 3072, 4096, 256, 64, 8
-Q = P // 4
 NG = (N - 1) * G
 GH = E + 16
 WEND = GH + 2 * NG + 16
@@ -13,10 +12,9 @@ FAR = [[4 * d + s for d in range(8) for s in range(4)
         if max(abs(2 * DX[d] + s % 2 - c % 2), abs(2 * DY[d] + s // 2 - c // 2)) > 1] for c in range(4)]
 
 XN_CHUNKS = 4
-XN_PRE = 1
 XN_MID = 3
-WT_ACT = 25
-WT_EARLY = 4
+WT_A = (10, 16, 16)
+FILL_V = 2304
 HALVES = (1, 2)
 SPREAD = (True, False)
 RELAY_ENGINES = 8
@@ -24,24 +22,17 @@ RELAY_ENGINES = 8
 SCRATCH = {
     "ex0": ("sbuf", [128, WEND], "bfloat16"),
     "ex1": ("sbuf", [128, WEND], "bfloat16"),
-    "kn": ("sbuf", [128, Q], "int32"),
-    "kf": ("sbuf", [128, Q + NG + 8], "float32"),
+    "kz": ("sbuf", [128, P + NG + 8], "int32"),
     "ng": ("sbuf", [128, NL // 16], "int32"),
-    "qi": ("sbuf", [128, NL // 16], "int32"),
-    "tq": ("sbuf", [128, NL // 16], "float32"),
-    "lo": ("sbuf", [128, NL // 16], "int32"),
-    "qu": ("sbuf", [128, NL // 16], "uint16"),
     "lu": ("sbuf", [128, NL // 16], "uint16"),
     "pi": ("sbuf", [128, 1], "int32"),
     "ix": ("sbuf", [128, NG + 8], "float32"),
     "ci": ("sbuf", [128, 8], "int32"),
     "cf": ("sbuf", [128, 8], "float32"),
     "ct": ("sbuf", [128, 8], "float32"),
-    "oh": ("sbuf", [128, 8], "float32"),
     "big": ("sbuf", [128, 2 * BW], "float16"),
     "i64f": ("sbuf", [128, 64], "float32"),
     "i64b": ("sbuf", [128, 64], "bfloat16"),
-    "mk": ("sbuf", [128, NL], "bfloat16"),
     "xs": ("sbuf", [128, NL], "float16"),
     "og0": ("sbuf", [128, NG // 8], "uint16"),
     "og1": ("sbuf", [128, NG // 8], "uint16"),
@@ -181,94 +172,112 @@ def rank_program(g, core, T, topo):
     py = (((T.py00, T.py01),), ((T.py10, T.py11), (T.pg0, T.pg1)))
     GC = NG // 16
 
-    m_ng, m_kid, m_tr, m_ex = mark(), mark(), mark(), (mark(), mark())
-    to(m_ng, S.dma_start(T.ng[:, 0:GC], T.give[:]), 16)
-    to(m_ng, A.dma_start(T.ng[:, GC:], T.near[:]), 16)
-    to(m_kid, S.dma_start(T.kn[:], T.kid[:]), 16)
-    for k in range(2):
-        to(m_ex[0], S.dma_start(ex[0][64 * k:64 * k + 64, 0:E], T.ex[0:64, :]), 16)
+    m_give, m_near, m_kid, m_tr, m_ex, m_fill = mark(), mark(), mark(), mark(), (mark(), mark()), mark()
+    m_pi = to(mark(), g.iota(T.pi[:], [[1, 1]], 0, 1))
+    to(m_fill, g.iota(T.kz[:, FILL_V:P], [[0, P - FILL_V]], E // 2, 0))
+    to(m_fill, V.memset(T.kz[:, 0:FILL_V], E // 2))
+    m_ix = to(mark(), g.iota(T.ix[:], [[1, NG + 8]], 0, 0, allow_small_or_imprecise_dtypes=True))
+    to(m_give, A.dma_start(T.ng[:, 0:GC], T.give[:]), 16)
     for w in range(2):
         for k in range(2):
-            to(m_tr, S.dma_start(T.trr[64 * k:64 * k + 64, w, :], T.tr[64 * w:64 * w + 64, :]), 16)
+            to(m_tr, (S, A)[k].dma_start(T.trr[64 * k:64 * k + 64, w, :], T.tr[64 * w:64 * w + 64, :]), 16)
+    to(m_near, A.dma_start(T.ng[:, GC:], T.near[:]), 16)
+    to(m_ex[0], S.dma_start(ex[0][0:64, 0:E], T.ex[0:64, :]), 16)
+    wait(S, m_fill)
+    to(m_kid, S.dma_start(T.kz[0::4, 0:P], T.kid[:]), 16)
+    to(m_ex[0], S.dma_start(ex[0][64:128, 0:E], T.ex[0:64, :]), 16)
     wait(S, m_kid)
     for k in range(2):
         to(m_ex[1], S.dma_start(ex[1][64 * k:64 * k + 64, 0:E], T.ex[64:128, :]), 16)
 
-    m_pi = to(mark(), g.iota(T.pi[:], [[1, 1]], 0, 1))
-    m_ix = to(mark(), g.iota(T.ix[:], [[1, NG + 8]], 0, 0, allow_small_or_imprecise_dtypes=True))
+    m_tf = to(mark(), V.memset(T.tf[:], 0.0))
+    wait(V, m_pi)
+    m = mark()
+    for j, b in enumerate((1, 4, 8, 48, 64, 63, 2)):
+        to(m, V.tensor_scalar(T.ci[:, j:j + 1], T.pi[:], b, None, op.bitwise_and))
     m_zero = mark()
     for w in range(2):
         to(m_zero, V.memset(ex[w][:, E:GH], 0.0))
         to(m_zero, V.memset(ex[w][:, WEND - 16:WEND], 0.0))
-    to(m_zero, V.memset(T.tf[:], 0.0))
-    wait(V, m_pi)
-    m = mark()
-    for j, b in enumerate((3, 4, 8, 48, 64, 63)):
-        to(m, V.tensor_scalar(T.ci[:, j:j + 1], T.pi[:], b, None, op.bitwise_and))
     wait(V, m)
-    m = to(mark(), V.tensor_copy(T.cf[:, 0:6], T.ci[:, 0:6]))
-    wait(V, m, m_ix)
-    cf = [T.cf[:, j:j + 1] for j in range(6)]
-    ct = [T.ct[:, j:j + 1] for j in range(4)]
-    m_oh = mark()
-    to(m_oh, V.tensor_scalar(ct[0], cf[1], 16.0, cf[3], op.mult, op.add))
-    to(m_oh, V.tensor_scalar(ct[1], cf[4], BW / 64.0, 14.0, op.mult, op.add))
-    to(m_oh, V.tensor_scalar(T.oh[:, 0:4], T.ix[:, 0:4], cf[0], None, op.is_equal))
-    to(m_oh, V.tensor_scalar(T.oh[:, 4:5], cf[0], 2.0, None, op.is_ge))
-    wait(V, m_oh)
+    m = to(mark(), V.tensor_copy(T.cf[:, 0:7], T.ci[:, 0:7]))
+    wait(V, m, m_ix, m_give)
+    cf = [T.cf[:, j:j + 1] for j in range(7)]
+    ct = [T.ct[:, j:j + 1] for j in range(5)]
     m = mark()
-    to(m, V.tensor_scalar(ct[2], cf[2], 0.125, ct[1], op.mult, op.add))
-    to(m, V.tensor_scalar(ct[3], T.oh[:, 3:4], cf[2], 0.125, op.mult, op.mult))
-    wait(V, m)
-    m_big = to(mark(), V.tensor_scalar(T.big[:], T.ix[:, 0:2 * BW], ct[0], ct[2], op.subtract, op.is_equal))
-    m_kf = to(mark(), V.tensor_scalar(T.kf[:, Q:], T.ix[:], ct[3], (GH - E // 2) / 2.0, op.add, op.add))
+    to(m, V.tensor_scalar(ct[0], cf[1], 16.0, cf[3], op.mult, op.add))
+    to(m, V.tensor_scalar(ct[1], cf[4], BW / 64.0, 14.0, op.mult, op.add))
+    to(m, V.tensor_scalar(ct[3], cf[0], cf[2], 0.125, op.mult, op.mult))
     m_i64 = mark()
     to(m_i64, V.tensor_scalar(T.i64f[:], T.ix[:, 0:64], cf[5], None, op.is_equal))
     to(m_i64, V.tensor_scalar(T.i64b[:], T.ix[:, 0:64], cf[5], None, op.is_equal))
+    m_lu = to(mark(), V.tensor_copy(T.lu[:, 0:GC], T.ng[:, 0:GC]))
+    wait(V, m)
+    m = mark()
+    to(m, V.tensor_scalar(ct[2], cf[2], 0.125, ct[1], op.mult, op.add))
+    to(m, V.tensor_scalar(ct[4], cf[6], 500.0, ct[0], op.mult, op.add))
+    m_ext = to(mark(), V.tensor_scalar(T.kz[:, P:], T.ix[:], ct[3], (GH + E // 2) / 2.0, op.add, op.add))
+    wait(V, m)
+    m_big = to(mark(), V.tensor_scalar(T.big[:], T.ix[:, 0:2 * BW], ct[4], ct[2], op.subtract, op.is_equal))
+    wait(V, m_near)
+    to(m_lu, V.tensor_copy(T.lu[:, GC:], T.ng[:, GC:]))
 
-    wait(V, m_ng)
-    m = to(mark(), V.tensor_scalar(T.qi[:], T.ng[:], 1.0 / Q, 0.5 / Q - 0.5, op.mult, op.add))
-    wait(V, m)
-    m_qu = to(mark(), V.tensor_copy(T.qu[:], T.qi[:]))
-    m = to(mark(), V.tensor_scalar(T.tq[:], T.qi[:], 3.0, -float(Q), op.min, op.mult))
-    wait(V, m)
-    m = to(mark(), V.tensor_tensor(T.lo[:], T.ng[:], T.tq[:], op.add))
-    wait(V, m)
-    m_lu = to(mark(), V.tensor_copy(T.lu[:], T.lo[:]))
+    wait(A, m_tr, m_tf)
+    m = mark()
+    for c in range(4):
+        for i0, p0, n in runs(c):
+            a = 32 * (c // 2) + p0
+            to(m, copy(A, T.tf[:, c % 2, :, a:a + n], T.trr[:, :, 27 * c + i0:27 * c + i0 + n]))
+    wait(A, m)
+    m_trw = mark()
+    for k in range(2):
+        to(m_trw, copy(A, T.trw[64 * k:64 * k + 64, :], T.tf[64 * k:64 * k + 64, :, :, k::2]))
+    m_wt = mark()
+    made = [0]
+
+    def blocks(q, n):
+        for e in range(made[0], made[0] + n):
+            dst = T.wt[:, 128 * e:128 * e + 128]
+            if q is V:
+                to(m_wt, V.tensor_scalar(dst, T.trw[:], T.i64b[:, e:e + 1], None, op.mult))
+            else:
+                to(m_wt, A.activation(dst, T.trw[:], Copy, scale=T.i64f[:, e:e + 1]))
+        made[0] += n
+
+    wait(A, m_trw, m_i64)
+    blocks(A, WT_A[0])
 
     cw = 8 * M // 16 // XN_CHUNKS
     spans = [(0, GC)] + [(GC + i * cw, GC + (i + 1) * cw) for i in range(XN_CHUNKS)]
-    wait(A, m_oh, m_qu)
-    m_mk = [to(mark(), A.activation(T.mk[:, 16 * a:16 * b], T.oh[:, 0:5].indirect(T.qu[:, a:b]), Copy))
-            for a, b in spans]
+    wait(V, m_kid, m_ext, m_lu)
 
-    wait(V, m_kid)
-    to(m_kf, V.tensor_scalar(T.kf[:, 0:Q], T.kn[:], -float(E // 2), None, op.add))
-    wait(V, m_kf, m_lu)
-
-    def lookup(i, m):
+    def lookup(i):
         a, b = spans[i]
-        wait(V, m_mk[i])
-        return to(m, V.tensor_tensor(T.xs[:, 16 * a:16 * b], T.kf[:].indirect(T.lu[:, a:b]),
-                                     T.mk[:, 16 * a:16 * b], op.mult))
+        return to(mark(), V.tensor_scalar(T.xs[:, 16 * a:16 * b], T.kz[:].indirect(T.lu[:, a:b]),
+                                          -float(E // 2), None, op.add))
 
-    def deal(ps, w, a, b):
+    def deal(ps, w, i):
+        a, b = spans[i]
         for u in range(8):
             c0 = BW * w + 14 - 2 * u
-            ins = PE.matmul(ps, T.big[:, c0:c0 + 128], T.xs[:, a + u:b:8], u == 0, u == 7)
-        return to(mark(), ins)
+            ins = PE.matmul(ps, T.big[:, c0:c0 + 128], T.xs[:, 16 * a + u:16 * b:8], u == 0, u == 7)
+        return ins
 
-    m_xg, m_xn = lookup(0, mark()), mark()
-    wait(PE, m_big, m_xg)
-    m_pg = [deal(pg[w][:, 0:NG // 8], w, 0, NG) for w in range(2)]
-    m_og = []
-    for w in range(2):
-        wait(V, m_pg[w])
-        m_og.append(to(mark(), V.tensor_scalar(og[w][:], pg[w][:, 0:NG // 8], float(E // 2), None, op.add)))
-    for i in range(XN_PRE):
-        lookup(1 + i, m_xn)
+    m_pn = (mark(), mark())
+
+    def near(i):
+        wait(PE, lookup(1 + i))
+        nd = 8 // XN_CHUNKS
+        for w in range(2):
+            to(m_pn[w], deal(pn[w][:, nd * i:nd * (i + 1), :], w, 1 + i))
+
+    wait(PE, m_big, lookup(0))
+    m_pg = [to(mark(), deal(pg[w][:, 0:NG // 8], w, 0)) for w in range(2)]
+    m_og = [None, None]
 
     def ghosts(w):
+        wait(V, m_pg[w])
+        m_og[w] = to(mark(), V.tensor_scalar(og[w][:], pg[w][:, 0:NG // 8], float(E // 2), None, op.add))
         for q in (V, A):
             wait(q, m_og[w], m_ex[w])
         sets = (sorted(x[0] for x in rel), sorted(x[0] for x in dire))
@@ -296,38 +305,15 @@ def rank_program(g, core, T, topo):
     for q in (V, A):
         wait(q, m_zero)
     ghosts(0)
-
-    wait(A, m_tr)
-    m = mark()
-    for c in range(4):
-        for i0, p0, n in runs(c):
-            a = 32 * (c // 2) + p0
-            to(m, copy(A, T.tf[:, c % 2, :, a:a + n], T.trr[:, :, 27 * c + i0:27 * c + i0 + n]))
-    wait(A, m)
-    m_trw = mark()
-    for k in range(2):
-        to(m_trw, copy(A, T.trw[64 * k:64 * k + 64, :], T.tf[64 * k:64 * k + 64, :, :, k::2]))
-
-    m_wt = mark()
-
-    def blocks(q, es):
-        for e in es:
-            dst = T.wt[:, 128 * e:128 * e + 128]
-            if q is V:
-                to(m_wt, V.tensor_scalar(dst, T.trw[:], T.i64b[:, e:e + 1], None, op.mult))
-            else:
-                to(m_wt, A.activation(dst, T.trw[:], Copy, scale=T.i64f[:, e:e + 1]))
-
-    wait(A, m_trw, m_i64)
-    blocks(A, range(0, WT_EARLY))
-    for i in range(XN_PRE, XN_PRE + XN_MID):
-        lookup(1 + i, m_xn)
+    blocks(A, WT_A[1])
+    for i in range(XN_MID):
+        near(i)
     ghosts(1)
-    for i in range(XN_PRE + XN_MID, XN_CHUNKS):
-        lookup(1 + i, m_xn)
-    blocks(A, range(WT_EARLY, WT_ACT))
-    wait(PE, m_xn)
-    m_pn = [deal(pn[w][:, 0:8, :], w, NG, NL) for w in range(2)]
+    for i in range(XN_MID, XN_CHUNKS):
+        near(i)
+    blocks(A, WT_A[2])
+    wait(V, m_trw, m_i64)
+    blocks(V, 4)
     m_on = []
     for w in range(2):
         wait(V, m_pn[w])
@@ -336,8 +322,7 @@ def rank_program(g, core, T, topo):
             to(m, V.tensor_scalar(on[w][:, 8 * hw * h:8 * hw * (h + 1)], pn[w][:, 0:8, hw * h:hw * (h + 1)],
                                   float(E // 2), None, op.add))
         m_on.append(m)
-    wait(V, m_trw, m_i64)
-    blocks(V, range(WT_ACT, 64))
+    blocks(V, 64 - made[0])
     wait(PE, m_wt)
 
     m_out = mark()

from concourse.bass import DstId, RemoteDMATransfer
from concourse.mybir import AluOpType, ActivationFunctionType

P, E, M, G, N = 3072, 4096, 256, 64, 8
NG = (N - 1) * G
GH = E + 16
WEND = GH + 2 * NG + 16
BW = 144
NL = NG + 8 * M
DX, DY = (-1, 0, 1, -1, 1, -1, 0, 1), (-1, -1, -1, 0, 0, 1, 1, 1)
FAR = [[4 * d + s for d in range(8) for s in range(4)
        if max(abs(2 * DX[d] + s % 2 - c % 2), abs(2 * DY[d] + s // 2 - c // 2)) > 1] for c in range(4)]

XN_CHUNKS = 4
XN_MID = 3
WT_A = (10, 16, 16)
FILL_V = 2304
HALVES = (1, 2)
SPREAD = (True, False)
RELAY_ENGINES = 8

SCRATCH = {
    "ex0": ("sbuf", [128, WEND], "bfloat16"),
    "ex1": ("sbuf", [128, WEND], "bfloat16"),
    "kz": ("sbuf", [128, P + NG + 8], "int32"),
    "ng": ("sbuf", [128, NL // 16], "int32"),
    "lu": ("sbuf", [128, NL // 16], "uint16"),
    "pi": ("sbuf", [128, 1], "int32"),
    "ix": ("sbuf", [128, NG + 8], "float32"),
    "ci": ("sbuf", [128, 8], "int32"),
    "cf": ("sbuf", [128, 8], "float32"),
    "ct": ("sbuf", [128, 8], "float32"),
    "big": ("sbuf", [128, 2 * BW], "float16"),
    "i64f": ("sbuf", [128, 64], "float32"),
    "i64b": ("sbuf", [128, 64], "bfloat16"),
    "xs": ("sbuf", [128, NL], "float16"),
    "og0": ("sbuf", [128, NG // 8], "uint16"),
    "og1": ("sbuf", [128, NG // 8], "uint16"),
    "on0": ("sbuf", [128, M], "uint16"),
    "on1": ("sbuf", [128, M], "uint16"),
    "gs0": ("sbuf", [128, 2 * NG], "bfloat16"),
    "gs1": ("sbuf", [128, 2 * NG], "bfloat16"),
    "rl0": ("sbuf", [128, 2 * G], "bfloat16"),
    "rl1": ("sbuf", [128, 2 * G], "bfloat16"),
    "trr": ("sbuf", [128, 2, 108], "bfloat16"),
    "tf": ("sbuf", [128, 2, 2, 64], "bfloat16"),
    "trw": ("sbuf", [128, 128], "bfloat16"),
    "wt": ("sbuf", [128, 64 * 128], "bfloat16"),
    "v0": ("sbuf", [128, 16 * M], "bfloat16"),
    "v1": ("sbuf", [128, 16 * M], "bfloat16"),
    "o0": ("sbuf", [128, 2 * M], "float32"),
    "o1": ("sbuf", [128, 2 * M], "float32"),
    "pg0": ("psum", [128, 512], "float32"),
    "pg1": ("psum", [128, 512], "float32"),
    "pn0": ("psum", [128, 16, 32], "float32"),
    "pn1": ("psum", [128, 16, 32], "float32"),
    "py00": ("psum", [128, 512], "float32"),
    "py01": ("psum", [128, 512], "float32"),
    "py10": ("psum", [128, 512], "float32"),
    "py11": ("psum", [128, 512], "float32"),
}
NSEM = 120
SEMAPHORES = ["arr0", "arr1", "rin0", "rin1", "sent"] + ["s%d" % i for i in range(NSEM)]


def bits(engs):
    m = 0
    for e in engs:
        m |= 1 << e
    return m


def pow2(n):
    p = 1
    while 2 * p <= n:
        p *= 2
    return p


def routes(cores, topo):
    out = []
    n = len(cores)
    for r, src in enumerate(cores):
        dsts = [(d, cores[(r + d) % n]) for d in range(1, n)]
        direct = [x for x in dsts if topo.may_write(src, x[1])]
        cross = [x for x in dsts if not topo.may_write(src, x[1])]
        cross.sort(key=lambda x: not topo.mates(src, x[1]))
        used, hand = [], []
        for d, dst in cross:
            able = [c for c in topo.cores_of(src) if c not in cores and c not in used and topo.may_write(c, dst)]
            able.sort(key=lambda c: topo.die(c) != topo.die(src))
            used.append(able[0])
            hand.append((d, able[0], dst))
        near = [h for h in hand if topo.die(h[1]) == topo.die(src)]
        far = [h for h in hand if topo.die(h[1]) != topo.die(src)]
        off = list(topo.engines(src, direct[0][1])) if direct else []
        mine = {h: [] for h in hand}
        for w in range(2):
            engs = [e for e in topo.engines(src, hand[0][1]) if SPREAD[w] or e not in off]
            pools = ((near, engs[1::2]), (far, engs[0::2])) if near and far else ((hand, engs),)
            for hs, pool in pools:
                k = pow2(len(pool) // len(hs))
                for i, h in enumerate(hs):
                    mine[h].append(pool[i * k:(i + 1) * k])
        rel = [(h[0], h[1], mine[h], h[2], topo.engines(h[1], h[2])[:RELAY_ENGINES]) for h in hand]
        dire = []
        for i, (d, dst) in enumerate(direct):
            left = len(direct) - i
            k = pow2(len(off) - (left - 1) * pow2(len(off) // left))
            dire.append((d, dst, off[:k]))
            off = off[k:]
        out.append((dire, rel))
    return out


def runs(c):
    f, out, i = FAR[c], [], 0
    while i < len(f):
        j = i
        while j + 1 < len(f) and f[j + 1] == f[j] + 1:
            j += 1
        out.append((i, f[i], j - i + 1))
        i = j + 1
    return out


def relay_program(g, core, T, topo, d, engs_in, dst, engs_out):
    rid, pid = topo.addr(dst, core)
    for w in range(2):
        g.wait_ge(T.sem["rin%d" % w], len(engs_in[w]))
        a = GH + 2 * G * (d - 1)
        g.remote_dma(T["ex%d" % w][:, a:a + 2 * G], T["rl%d" % w][:], T.sem["arr%d" % w], T.sem.sent,
                     pid, rid, bits(engs_out))
    g.wait_ge(T.sem.sent, 2 * len(engs_out))


def rank_program(g, core, T, topo):
    plan = routes(list(T.cores), topo)
    rank = T.rank_of(core)
    if rank is None:
        for dire, rel in plan:
            for d, c, engs_in, dst, engs_out in rel:
                if c == core:
                    relay_program(g, core, T, topo, d, engs_in, dst, engs_out)
        return
    dire, rel = plan[rank]
    arrive = sum(len(x[2]) for p in plan for x in p[0] if x[1] == core) \
        + sum(len(x[4]) for p in plan for x in p[1] if x[3] == core)

    V, A, PE, S = g.vector, g.scalar, g.tensor, g.sync
    op, Copy = AluOpType, ActivationFunctionType.Copy
    count = [0]

    def mark():
        count[0] += 1
        return [T.sem["s%d" % (count[0] - 1)], 0]

    def to(m, ins, n=1):
        ins.then_inc(m[0], n)
        m[1] += n
        return m

    def wait(q, *ms):
        for m in ms:
            q.wait_ge(m[0], m[1])

    def copy(q, dst, src):
        return V.tensor_copy(dst, src) if q is V else A.activation(dst, src, Copy)

    ex, gs, og, on = (T.ex0, T.ex1), (T.gs0, T.gs1), (T.og0, T.og1), (T.on0, T.on1)
    vv, oo, pg, pn = (T.v0, T.v1), (T.o0, T.o1), (T.pg0, T.pg1), (T.pn0, T.pn1)
    py = (((T.py00, T.py01),), ((T.py10, T.py11), (T.pg0, T.pg1)))
    GC = NG // 16

    m_give, m_near, m_kid, m_tr, m_ex, m_fill = mark(), mark(), mark(), mark(), (mark(), mark()), mark()
    m_pi = to(mark(), g.iota(T.pi[:], [[1, 1]], 0, 1))
    to(m_fill, g.iota(T.kz[:, FILL_V:P], [[0, P - FILL_V]], E // 2, 0))
    to(m_fill, V.memset(T.kz[:, 0:FILL_V], E // 2))
    m_ix = to(mark(), g.iota(T.ix[:], [[1, NG + 8]], 0, 0, allow_small_or_imprecise_dtypes=True))
    to(m_give, A.dma_start(T.ng[:, 0:GC], T.give[:]), 16)
    for w in range(2):
        for k in range(2):
            to(m_tr, (S, A)[k].dma_start(T.trr[64 * k:64 * k + 64, w, :], T.tr[64 * w:64 * w + 64, :]), 16)
    to(m_near, A.dma_start(T.ng[:, GC:], T.near[:]), 16)
    to(m_ex[0], S.dma_start(ex[0][0:64, 0:E], T.ex[0:64, :]), 16)
    wait(S, m_fill)
    to(m_kid, S.dma_start(T.kz[0::4, 0:P], T.kid[:]), 16)
    to(m_ex[0], S.dma_start(ex[0][64:128, 0:E], T.ex[0:64, :]), 16)
    wait(S, m_kid)
    for k in range(2):
        to(m_ex[1], S.dma_start(ex[1][64 * k:64 * k + 64, 0:E], T.ex[64:128, :]), 16)

    m_tf = to(mark(), V.memset(T.tf[:], 0.0))
    wait(V, m_pi)
    m = mark()
    for j, b in enumerate((1, 4, 8, 48, 64, 63, 2)):
        to(m, V.tensor_scalar(T.ci[:, j:j + 1], T.pi[:], b, None, op.bitwise_and))
    m_zero = mark()
    for w in range(2):
        to(m_zero, V.memset(ex[w][:, E:GH], 0.0))
        to(m_zero, V.memset(ex[w][:, WEND - 16:WEND], 0.0))
    wait(V, m)
    m = to(mark(), V.tensor_copy(T.cf[:, 0:7], T.ci[:, 0:7]))
    wait(V, m, m_ix, m_give)
    cf = [T.cf[:, j:j + 1] for j in range(7)]
    ct = [T.ct[:, j:j + 1] for j in range(5)]
    m = mark()
    to(m, V.tensor_scalar(ct[0], cf[1], 16.0, cf[3], op.mult, op.add))
    to(m, V.tensor_scalar(ct[1], cf[4], BW / 64.0, 14.0, op.mult, op.add))
    to(m, V.tensor_scalar(ct[3], cf[0], cf[2], 0.125, op.mult, op.mult))
    m_i64 = mark()
    to(m_i64, V.tensor_scalar(T.i64f[:], T.ix[:, 0:64], cf[5], None, op.is_equal))
    to(m_i64, V.tensor_scalar(T.i64b[:], T.ix[:, 0:64], cf[5], None, op.is_equal))
    m_lu = to(mark(), V.tensor_copy(T.lu[:, 0:GC], T.ng[:, 0:GC]))
    wait(V, m)
    m = mark()
    to(m, V.tensor_scalar(ct[2], cf[2], 0.125, ct[1], op.mult, op.add))
    to(m, V.tensor_scalar(ct[4], cf[6], 500.0, ct[0], op.mult, op.add))
    m_ext = to(mark(), V.tensor_scalar(T.kz[:, P:], T.ix[:], ct[3], (GH + E // 2) / 2.0, op.add, op.add))
    wait(V, m)
    m_big = to(mark(), V.tensor_scalar(T.big[:], T.ix[:, 0:2 * BW], ct[4], ct[2], op.subtract, op.is_equal))
    wait(V, m_near)
    to(m_lu, V.tensor_copy(T.lu[:, GC:], T.ng[:, GC:]))

    wait(A, m_tr, m_tf)
    m = mark()
    for c in range(4):
        for i0, p0, n in runs(c):
            a = 32 * (c // 2) + p0
            to(m, copy(A, T.tf[:, c % 2, :, a:a + n], T.trr[:, :, 27 * c + i0:27 * c + i0 + n]))
    wait(A, m)
    m_trw = mark()
    for k in range(2):
        to(m_trw, copy(A, T.trw[64 * k:64 * k + 64, :], T.tf[64 * k:64 * k + 64, :, :, k::2]))
    m_wt = mark()
    made = [0]

    def blocks(q, n):
        for e in range(made[0], made[0] + n):
            dst = T.wt[:, 128 * e:128 * e + 128]
            if q is V:
                to(m_wt, V.tensor_scalar(dst, T.trw[:], T.i64b[:, e:e + 1], None, op.mult))
            else:
                to(m_wt, A.activation(dst, T.trw[:], Copy, scale=T.i64f[:, e:e + 1]))
        made[0] += n

    wait(A, m_trw, m_i64)
    blocks(A, WT_A[0])

    cw = 8 * M // 16 // XN_CHUNKS
    spans = [(0, GC)] + [(GC + i * cw, GC + (i + 1) * cw) for i in range(XN_CHUNKS)]
    wait(V, m_kid, m_ext, m_lu)

    def lookup(i):
        a, b = spans[i]
        return to(mark(), V.tensor_scalar(T.xs[:, 16 * a:16 * b], T.kz[:].indirect(T.lu[:, a:b]),
                                          -float(E // 2), None, op.add))

    def deal(ps, w, i):
        a, b = spans[i]
        for u in range(8):
            c0 = BW * w + 14 - 2 * u
            ins = PE.matmul(ps, T.big[:, c0:c0 + 128], T.xs[:, 16 * a + u:16 * b:8], u == 0, u == 7)
        return ins

    m_pn = (mark(), mark())

    def near(i):
        wait(PE, lookup(1 + i))
        nd = 8 // XN_CHUNKS
        for w in range(2):
            to(m_pn[w], deal(pn[w][:, nd * i:nd * (i + 1), :], w, 1 + i))

    wait(PE, m_big, lookup(0))
    m_pg = [to(mark(), deal(pg[w][:, 0:NG // 8], w, 0)) for w in range(2)]
    m_og = [None, None]

    def ghosts(w):
        wait(V, m_pg[w])
        m_og[w] = to(mark(), V.tensor_scalar(og[w][:], pg[w][:, 0:NG // 8], float(E // 2), None, op.add))
        for q in (V, A):
            wait(q, m_og[w], m_ex[w])
        sets = (sorted(x[0] for x in rel), sorted(x[0] for x in dire))
        ms = (mark(), mark())
        for ds, m in zip(sets, ms):
            cols = [8 * (d - 1) + 4 * h for d in ds for h in range(2)]
            for q, mine in ((V, cols[:len(ds)]), (A, cols[len(ds):])):
                while mine:
                    n = 1
                    while n < len(mine) and mine[n] == mine[0] + 4 * n:
                        n += 1
                    a, b, mine = mine[0], mine[0] + 4 * n, mine[n:]
                    to(m, copy(q, gs[w][:, 16 * a:16 * b], ex[w][:, 0:GH].indirect(og[w][:, a:b])))
        blk = lambda d: gs[w][:, 2 * G * (d - 1):2 * G * d]
        ident = lambda c: DstId(rid=topo.addr(c, core)[0], pnc=topo.addr(c, core)[1])
        wait(g, ms[0])
        g.remote_dma_fused([RemoteDMATransfer(dst_ids=[ident(c)], dma_engine_mask=bits(e[w]), remote_sem=T.sem["rin%d" % w],
                                              src=blk(d), dst=T["rl%d" % w][:]) for d, c, e, _, _ in rel],
                           local_sem=T.sem.sent)
        wait(g, ms[1])
        g.remote_dma_fused([RemoteDMATransfer(dst_ids=[ident(c)], dma_engine_mask=bits(e), remote_sem=T.sem["arr%d" % w],
                                              src=blk(d), dst=ex[w][:, GH + 2 * G * (d - 1):GH + 2 * G * d])
                            for d, c, e in dire], local_sem=T.sem.sent)

    for q in (V, A):
        wait(q, m_zero)
    ghosts(0)
    blocks(A, WT_A[1])
    for i in range(XN_MID):
        near(i)
    ghosts(1)
    for i in range(XN_MID, XN_CHUNKS):
        near(i)
    blocks(A, WT_A[2])
    wait(V, m_trw, m_i64)
    blocks(V, 4)
    m_on = []
    for w in range(2):
        wait(V, m_pn[w])
        m, hw = mark(), 32 // HALVES[w]
        for h in range(HALVES[w]):
            to(m, V.tensor_scalar(on[w][:, 8 * hw * h:8 * hw * (h + 1)], pn[w][:, 0:8, hw * h:hw * (h + 1)],
                                  float(E // 2), None, op.add))
        m_on.append(m)
    blocks(V, 64 - made[0])
    wait(PE, m_wt)

    m_out = mark()

    def store(w, h, done):
        mh = M // HALVES[w]
        for cp, q, dq in ((0, V, S), (1, A, A)):
            b = M * cp + mh * h
            wait(q, done[cp])
            wait(dq, to(mark(), copy(q, oo[w][:, b:b + mh], py[w][h][cp][:, 0:mh])))
            if HALVES[w] == 1:
                to(m_out, dq.dma_start(T.y[64 * w:64 * w + 64, 2 * M * cp:2 * M * (cp + 1)], oo[w][:, b:b + mh]), 16)
            else:
                for c in range(2):
                    a = 2 * M * cp + M * c + mh * h
                    to(m_out, dq.dma_start(T.y[64 * w:64 * w + 64, a:a + mh], oo[w][c::2, b:b + mh]), 16)

    pending, turn = [], 0
    for w in range(2):
        for q in (V, A):
            wait(q, m_on[w])
            q.wait_ge(T.sem["arr%d" % w], arrive)
        H = HALVES[w]
        mh, hw = M // H, 32 // H
        passes = [[(d, s) for d in range(8) for s in range(2)
                   if any(4 * d + 2 * s + k in FAR[c + 2 * cp] for k in range(2) for c in range(2))] for cp in range(2)]
        for h in range(H):
            done = [None, None]
            for n in range(8 // H):
                base = 8 * hw * h + 32 * n
                m = mark()
                if base == (0 if w == 0 else M - 32):
                    parts = ((V, 0, 16), (A, 16, 32))
                else:
                    parts = (((A, V)[turn], 0, 32),)
                    turn = 1 - turn
                for q, a, b in parts:
                    to(m, copy(q, vv[w][:, 16 * (base + a):16 * (base + b)],
                               ex[w][:].indirect(on[w][:, base + a:base + b])))
                if pending and n == min(3, 8 // H - 2):
                    store(*pending.pop())
                wait(PE, m)
                for cp in range(2):
                    for d in range(H * n, H * (n + 1)):
                        for s in range(2):
                            if (d, s) in passes[cp]:
                                j = ((2 * w + cp) * 8 + d) * 2 + s
                                a = 16 * (8 * hw * h + hw * d)
                                ins = PE.matmul(py[w][h][cp][:, 0:mh], T.wt[:, j::64],
                                                vv[w][:, a + s:a + 2 * mh:2],
                                                (d, s) == passes[cp][0], (d, s) == passes[cp][-1])
                                if (d, s) == passes[cp][-1]:
                                    done[cp] = to(mark(), ins)
            pending.append((w, h, done))
    store(*pending.pop())
    wait(S, m_out)
    g.wait_ge(T.sem.sent, sum(len(x[2][0]) + len(x[2][1]) for x in rel) + 2 * sum(len(x[2]) for x in dire))
